import numpy as np, ml_dtypes
CORES = [61,69,101,62,70,102]
N = 6
import mx_ref
NC, K, S = 512, 2, 1
CNT = [[128,232,0,0,136,16],[0,0,152,224,0,136],[24,0,208,256,24,0],[136,144,0,24,0,208],[48,0,152,0,304,8],[176,136,0,8,48,144]]
OFF = [[sum(c[:f]) for f in range(N + 1)] for c in CNT]
BF = ml_dtypes.bfloat16
def setup_inputs(rng):
    def f(*shape):
        return mx_ref.flush((rng.standard_normal(shape, dtype=np.float32) * np.exp2(rng.integers(-2, 3, shape[:-1] + (1,)))).astype(BF))
    return {"w": f(N, 128, 512), "x": f(N, 128, 4 * NC)}
def setup_inputs_blocks(rng):
    d = setup_inputs(rng)
    for k in ("w", "x"): d[k] = mx_ref.spread(d[k], rng, 4)
    return d
def setup_inputs_wide(rng):
    d = setup_inputs(rng)
    for k in ("w", "x"): d[k] = mx_ref.flush((d[k].astype(np.float32) * np.exp2(rng.integers(-8, 9, (N, 1, 1))).astype(np.float32)).astype(BF))
    return d
def setup_inputs_zeros(rng):
    d = setup_inputs(rng); v = d["x"].reshape(N, 128, -1, 4).copy()
    v[np.broadcast_to((rng.random((N, 1, v.shape[2], 1)) < 0.33), v.shape)] = 0
    d["x"] = v.reshape(d["x"].shape)
    return d
def reference(w, x):
    y = np.zeros((N, 128, K * NC), np.float32)
    for e in range(N):
        qw = mx_ref.quantize(w[e])
        for k in range(K):
            f = (e - S * k) % N
            t = np.concatenate([x[j][:, 4 * OFF[j][f]:4 * OFF[j][f + 1]] for j in range(N)], axis=1)
            y[e][:, NC * k:NC * k + NC] = mx_ref.matmul(qw, mx_ref.quantize(t))
    return {"y": y}

from concourse.bass import DstId, RemoteDMATransfer
from concourse.mybir import dt, ActivationFunctionType

N = 6
NC = 512
MINW = 128
BANK = 512
LAND = 1280
NPIECE, NARR, NGRP = 4, 12, 8
PAD = 48
SPLIT = True

SCRATCH = {
    "xt": ("sbuf", [128, 4 * NC], "bfloat16"),
    "wt": ("sbuf", [128, 512], "bfloat16"),
    "qx": ("sbuf", [128, NC], "float8_e4m3fn_x4"),
    "sx": ("sbuf", [128, NC], "uint8"),
    "qw": ("sbuf", [128, 128], "float8_e4m3fn_x4"),
    "sw": ("sbuf", [128, 128], "uint8"),
    "ql": ("sbuf", [128, LAND], "float8_e4m3fn_x4"),
    "sl": ("sbuf", [128, LAND], "uint8"),
    "ps": ("psum", [128, BANK * NGRP], "float32"),
    "yo": ("sbuf", [128, 2 * NC], "float32"),
}
SEMAPHORES = (["ld%d" % i for i in range(NPIECE)] + ["qz%d" % i for i in range(NPIECE)] + ["ldw", "qzw"]
              + ["ar%d" % i for i in range(NARR)] + ["mm%d" % i for i in range(NGRP)] + ["cp%d" % i for i in range(NGRP)]
              + ["sta", "stb", "sent"])


def _bits(mask):
    return [i for i in range(16) if (mask >> i) & 1]


def _mask(bits):
    m = 0
    for b in bits:
        m |= 1 << b
    return m


def _w(r):
    return r[1] - r[0]


def _fuse(items, key):
    calls, where = [], {}
    for it in items:
        k = key(it)
        if k in where and len(calls[where[k]]) < 4:
            calls[where[k]].append(it)
        else:
            where[k] = len(calls)
            calls.append([it])
    return calls


def _set_masks(topo, core, calls):
    dsts = [x["dst"] for c in calls for x in c]
    off = [d for d in dsts if topo.chip(d) != topo.chip(core)]
    offbits = _bits(topo.mask(core, off[0])) if off else []
    for c in calls:
        for far in (True, False):
            xs = [x for x in c if (topo.chip(x["dst"]) != topo.chip(core)) == far]
            if not xs:
                continue
            pool = offbits if far else [b for b in _bits(topo.mask(core, xs[0]["dst"])) if b not in offbits]
            per = 1
            while per * 2 * len(xs) <= len(pool):
                per *= 2
            for i, x in enumerate(xs):
                x["mask"] = _mask(pool[i * per:(i + 1) * per])
                x["eng"] = per


def _plan(CNT, cores, topo):
    n = len(cores)
    chip = [topo.chip(c) for c in cores]
    ybase = [[sum(CNT[i][f] for i in range(j)) for j in range(n)] for f in range(n)]
    pos, nat0 = [], []
    for j in range(n):
        row = CNT[j]
        cand = [s for s in range(n) if row[s - 1] == 0 or row[s] == 0]
        s = cand[0] if cand else j
        p, c = {}, 0
        for k in range(n):
            f = (s + k) % n
            p[f] = c
            c += row[f]
        pos.append(p)
        nat0.append(sum(row[:s]))
    flow, own = {}, {}
    for j in range(n):
        for e in range(n):
            segs = []
            for f in ((e - 1) % n, e):
                if CNT[j][f]:
                    a = pos[j][f]
                    if segs and segs[-1][1] == a:
                        segs[-1][1] = a + CNT[j][f]
                    else:
                        segs.append([a, a + CNT[j][f]])
            if j == e:
                own[e] = segs
            elif segs:
                assert len(segs) == 1
                flow[j, e] = segs[0]
    clusters = []
    for j in range(n):
        fs = [e for e in range(n) if (j, e) in flow and not topo.may_write(cores[j], cores[e])]
        for e in sorted(fs, key=lambda e: flow[j, e][0]):
            r = flow[j, e]
            if clusters and clusters[-1]["j"] == j and r[0] < clusters[-1]["b"]:
                clusters[-1]["es"].append(e)
                clusters[-1]["b"] = max(clusters[-1]["b"], r[1])
            else:
                clusters.append({"j": j, "es": [e], "a": r[0], "b": r[1]})
    relayed = set((cl["j"], e) for cl in clusters for e in cl["es"])
    sets = [[(cl["j"], e) for e in cl["es"]] for cl in clusters]
    sets += [[k for k in flow if k[0] == j and k not in relayed] for j in range(n)]
    for keys in sets:
        for k1 in keys:
            for k2 in keys:
                r1, r2 = flow[k1], flow[k2]
                if r2[0] <= r1[0] and r1[1] <= r2[1] and 0 < _w(r2) - _w(r1) <= PAD:
                    flow[k1] = list(r2)
    port = {}
    for (j, e), r in flow.items():
        if (j, e) not in relayed and chip[j] != chip[e]:
            k = (chip[e], topo.die(cores[j]))
            port[k] = port.get(k, 0) + 0.5 * _w(r)
    used = set(cores)
    everyone = range(topo.CORES_PER_CHIP * topo.CHIPS)
    for cl in sorted(clusters, key=lambda cl: -sum(_w(flow[cl["j"], e]) for e in cl["es"])):
        j = cl["j"]
        add = {}
        for e in cl["es"]:
            add[chip[e]] = add.get(chip[e], 0) + _w(flow[j, e])
        cands = [c for c in everyone if topo.chip(c) == chip[j] and c not in used
                 and all(topo.may_write(c, cores[e]) for e in cl["es"])]
        h = min(cands, key=lambda c: (max(port.get((ch, topo.die(c)), 0) + v for ch, v in add.items()), c))
        used.add(h)
        cl["h"] = h
        for ch, v in add.items():
            port[ch, topo.die(h)] = port.get((ch, topo.die(h)), 0) + v
    src, units = [], []
    for j in range(n):
        mine = [k for k in flow if k[0] == j]
        cuts = [0]
        for x in sorted(set(pos[j][f] for f in range(n) if CNT[j][f])):
            if x - cuts[-1] < MINW or NC - x < MINW:
                continue
            if all(not (flow[k][0] < x < flow[k][1]) or (x - flow[k][0] >= MINW and flow[k][1] - x >= MINW) for k in mine):
                cuts.append(x)
        cuts.append(NC)
        pieces = [(cuts[i], cuts[i + 1]) for i in range(len(cuts) - 1)]

        def klass(k):
            if k in relayed:
                return 0
            if chip[k[0]] == chip[k[1]]:
                return 3
            return 2 if topo.same_plane(chip[k[0]], chip[k[1]]) else 1

        def score(p):
            ov = [0, 0, 0, 0]
            for k in mine:
                ov[klass(k)] += max(0, min(p[1], flow[k][1]) - max(p[0], flow[k][0]))
            return [-v for v in ov]
        pieces.sort(key=score)

        def ready(a, b):
            return max(i for i, p in enumerate(pieces) if p[0] < b and a < p[1])
        legs = []
        for cl in clusters:
            if cl["j"] != j:
                continue
            cl["legs"] = []
            for p in (pieces if SPLIT else [(0, NC)]):
                a, b = max(cl["a"], p[0]), min(cl["b"], p[1])
                if a < b:
                    legs.append({"a": a, "b": b, "dst": cl["h"], "dcol": a, "cls": 0, "cl": cl})
        for k in mine:
            if k not in relayed:
                u = {"j": j, "e": k[1], "a": flow[k][0], "b": flow[k][1], "dst": cores[k[1]], "cls": klass(k)}
                legs.append(u)
                units.append(u)
        for x in legs:
            x["ready"] = ready(x["a"], x["b"])
        legs.sort(key=lambda x: (x["ready"], x["cls"], -_w((x["a"], x["b"]))))
        calls = _fuse(legs, lambda x: (x["ready"], x["b"] - x["a"]))
        _set_masks(topo, cores[j], calls)
        for ci, c in enumerate(calls):
            for x in c:
                x["eta"] = x["ready"] + ci + (2.0, 3.5, 3.0, 2.0)[x["cls"]] + (x["b"] - x["a"]) / 200.0
                if x["cls"] == 0:
                    k = len(x["cl"]["legs"])
                    x["sems"] = ("ar%d" % (2 * k), "ar%d" % (2 * k + 1))
                    x["cl"]["legs"].append(x)
        src.append({"pieces": pieces, "calls": calls})
    helper = {}
    for cl in clusters:
        j, outs = cl["j"], []
        for e in cl["es"]:
            r = flow[j, e]
            parts = [(max(r[0], x["a"]), min(r[1], x["b"])) for x in cl["legs"]] if SPLIT else [tuple(r)]
            for a, b in parts:
                if a < b:
                    need = [k for k, x in enumerate(cl["legs"]) if x["a"] < b and a < x["b"]]
                    outs.append({"j": j, "e": e, "a": a, "b": b, "dst": cores[e], "need": need})
        outs.sort(key=lambda u: (max(u["need"]), -(u["b"] - u["a"])))
        calls = _fuse(outs, lambda u: (max(u["need"]), u["b"] - u["a"]))
        _set_masks(topo, cl["h"], calls)
        for ci, c in enumerate(calls):
            for u in c:
                u["eta"] = max(cl["legs"][k]["eta"] for k in u["need"]) + 3.0 + ci + 3.5 + (u["b"] - u["a"]) / 200.0
                units.append(u)
        helper[cl["h"]] = {"calls": calls, "legs": cl["legs"]}
    dst = []
    for e in range(n):
        def outcols(j, a, b, col0):
            res = []
            for blk, f in ((0, e), (1, (e - 1) % n)):
                lo, hi = max(a, pos[j][f]), min(b, pos[j][f] + CNT[j][f])
                if lo < hi:
                    res.append((col0 + lo - a, blk * NC + ybase[f][j] + lo - pos[j][f], hi - lo))
            return res
        groups = []
        for a, b in own[e]:
            wa = a if b - a >= MINW else min(a, NC - MINW)
            wb = max(b, wa + MINW)
            groups.append({"own": True, "wa": wa, "wb": wb, "cp": outcols(e, a, b, a - wa), "sem": None})
        mine = sorted([u for u in units if u["e"] == e], key=lambda u: u["eta"])
        packs, cur = [], []
        for u in mine:
            if cur and sum(x["b"] - x["a"] for x in cur) + u["b"] - u["a"] > BANK:
                packs.append(cur)
                cur = []
            cur.append(u)
            if sum(x["b"] - x["a"] for x in cur) >= MINW:
                packs.append(cur)
                cur = []
        if cur:
            packs.append(cur)
        col = 0
        for gi, pk in enumerate(packs):
            ga = col
            for u in pk:
                u["dcol"] = col
                u["sems"] = ("ar%d" % gi, "ar%d" % gi)
                col += u["b"] - u["a"]
            wa = min(ga, col - MINW)
            assert wa >= 0 and col <= LAND
            cp = []
            for u in pk:
                cp += outcols(u["j"], u["a"], u["b"], u["dcol"] - wa)
            groups.append({"own": False, "wa": wa, "wb": col, "cp": cp, "sem": "ar%d" % gi,
                           "count": 2 * sum(u["eng"] for u in pk)})
        assert len(groups) <= NGRP
        dst.append(groups)
    return {"pos": pos, "nat0": nat0, "src": src, "helper": helper, "dst": dst}


def _send(g, T, topo, call, kind, codes, plane):
    trs = []
    for x in call:
        a, b, d = x["a"], x["b"], x["dcol"]
        if kind == 0:
            s_ap, d_ap = plane[:, a:b], T.sl[:, d:d + b - a]
        else:
            s_ap, d_ap = codes[:, a:b].bitcast(dt.uint8), T.ql[:, d:d + b - a].bitcast(dt.uint8)
        rid, pid, _ = topo.addr(x["dst"])
        trs.append((s_ap, d_ap, rid, pid, x["mask"], T.sem[x["sems"][kind]]))
    if len(trs) == 1:
        s_ap, d_ap, rid, pid, m, sem = trs[0]
        g.remote_dma(out_ap=d_ap, in_ap=s_ap, remote_sem=sem, local_sem=T.sem.sent, pid=pid, routing_id=rid,
                     dma_engine_mask=m)
    else:
        g.remote_dma_fused([RemoteDMATransfer(dst_ids=[DstId(rid=rid, pnc=pid)], dma_engine_mask=m, remote_sem=sem,
                                              src=s_ap, dst=d_ap) for s_ap, d_ap, rid, pid, m, sem in trs],
                           local_sem=T.sem.sent)
    return sum(x["eng"] for x in call)


def rank_program(g, core, T, topo):
    plan = _plan(T.tables["CNT"], list(T.cores), topo)
    if core in plan["helper"]:
        h = plan["helper"][core]
        sent = 0
        for call in h["calls"]:
            need = sorted(set(k for u in call for k in u["need"]))
            for kind in (0, 1):
                for k in need:
                    g.wait_ge(T.sem[h["legs"][k]["sems"][kind]], h["legs"][k]["eng"])
                sent += _send(g, T, topo, call, kind, T.ql, T.sl)
        g.wait_ge(T.sem.sent, sent)
        return
    rank = T.rank_of(core)
    if rank is None:
        return
    me, groups, n0 = plan["src"][rank], plan["dst"][rank], plan["nat0"][rank]
    dmaq = [g.sync, g.scalar]
    nld = []
    for i, (a, b) in enumerate(me["pieces"]):
        s = (n0 + a) % NC
        parts = [(a, b, s)] if s + b - a <= NC else [(a, a + NC - s, s), (a + NC - s, b, 0)]
        for pa, pb, ps in parts:
            dmaq[i % 2].dma_start(T.xt[:, 4 * pa:4 * pb], T.x[:, 4 * ps:4 * (ps + pb - pa)]).then_inc(T.sem["ld%d" % i], 16)
        nld.append(16 * len(parts))
    dmaq[len(me["pieces"]) % 2].dma_start(T.wt[:], T.w[:]).then_inc(T.sem.ldw, 16)
    for i, (a, b) in enumerate(me["pieces"]):
        g.vector.wait_ge(T.sem["ld%d" % i], nld[i])
        g.vector.quantize_mx(T.qx[:, a:b], T.sx[:, a:b], T.xt[:, 4 * a:4 * b]).then_inc(T.sem["qz%d" % i], 1)
    g.vector.wait_ge(T.sem.ldw, 16)
    g.vector.quantize_mx(T.qw[:], T.sw[:], T.wt[:]).then_inc(T.sem.qzw, 1)
    sent, seen = 0, -1
    for call in me["calls"]:
        while seen < call[0]["ready"]:
            seen += 1
            g.wait_ge(T.sem["qz%d" % seen], 1)
        for kind in (0, 1):
            sent += _send(g, T, topo, call, kind, T.qx, T.sx)
    while seen < len(me["pieces"]) - 1:
        seen += 1
        g.wait_ge(T.sem["qz%d" % seen], 1)
    g.wait_ge(T.sem.sent, sent)
    g.tensor.wait_ge(T.sem.qzw, 1)
    nst = [0, 0]
    stsem = [T.sem.sta, T.sem.stb]
    for k, gr in enumerate(groups):
        wa, wb = gr["wa"], gr["wb"]
        if gr["own"]:
            for i, p in enumerate(me["pieces"]):
                if p[0] < wb and wa < p[1]:
                    g.tensor.wait_ge(T.sem["qz%d" % i], 1)
            rhs, rsc = T.qx[:, wa:wb], T.sx[:, wa:wb]
        else:
            g.tensor.wait_ge(T.sem[gr["sem"]], gr["count"])
            rhs, rsc = T.ql[:, wa:wb], T.sl[:, wa:wb]
        g.tensor.matmul_mx(T.ps[:, BANK * k:BANK * k + wb - wa], T.qw[:], T.sw[:], rhs, rsc, True, True).then_inc(
            T.sem["mm%d" % k], 1)
        eng = g.vector if k % 2 == 0 else g.scalar
        eng.wait_ge(T.sem["mm%d" % k], 1)
        for pc, yc, w in gr["cp"]:
            o, i_ = T.yo[:, yc:yc + w], T.ps[:, BANK * k + pc:BANK * k + pc + w]
            if k % 2 == 0:
                g.vector.tensor_copy(o, i_).then_inc(T.sem["cp%d" % k], 1)
            else:
                g.scalar.activation(o, i_, ActivationFunctionType.Copy).then_inc(T.sem["cp%d" % k], 1)
        spans = []
        for _, yc, w in sorted(gr["cp"], key=lambda c: c[1]):
            if spans and spans[-1][1] == yc:
                spans[-1][1] = yc + w
            else:
                spans.append([yc, yc + w])
        spans.sort(key=lambda s: s[0] - s[1])
        for q in range(min(2, len(spans))):
            dmaq[q].wait_ge(T.sem["cp%d" % k], len(gr["cp"]))
        for i, (a, b) in enumerate(spans):
            dmaq[i % 2].dma_start(T.y[:, a:b], T.yo[:, a:b]).then_inc(stsem[i % 2], 16)
            nst[i % 2] += 16
    for q in (0, 1):
        if nst[q]:
            dmaq[q].wait_ge(stsem[q], nst[q])
